import numpy as np
import ml_dtypes


def mxq(x, axis, fmt="e4m3"):
    dtype, down = {"e4m3": (ml_dtypes.float8_e4m3fn, 7), "e5m2": (ml_dtypes.float8_e5m2, 14)}[fmt]
    v = np.moveaxis(np.asarray(x, np.float32).astype(ml_dtypes.bfloat16).astype(np.float64), axis, -1)
    blocks = v.reshape(v.shape[:-1] + (-1, 32))
    amax = np.abs(blocks).max(-1, keepdims=True)
    byte = np.maximum(np.where(amax > 0, np.frexp(amax)[1] - 1 + 127, 0) - down, 1)
    scale = np.exp2(byte - 127.0)
    codes = (blocks / scale).astype(np.float32).astype(dtype).astype(np.float64)
    return np.moveaxis((codes * scale).reshape(v.shape), -1, axis)


WIDE = False


def mx_kscale(k):
    if not WIDE:
        return np.ones(k)
    levels = np.array([10, -10, 5, -5, 0])
    if k % 512:
        return np.exp2(np.random.permutation(np.resize(levels, k // 32))).repeat(32)
    a = np.empty((k // 512, 16))
    for p in range(k // 512):
        a[p, :8] = np.random.permutation(np.resize(levels, 8))
        for g in range(8):
            far = levels[np.abs(levels - a[p, g]) >= 10]
            a[p, g + 8] = far[np.random.randint(len(far))]
    return np.exp2(a.ravel()).repeat(32)


def f64(x):
    return np.asarray(x).astype(np.float64)


def striped(idx):
    return np.tile(idx.reshape(-1, 16).T, (8, 1)).astype(np.uint16)


def unstriped(offs):
    return offs[:16].T.reshape(-1).astype(np.int64)


def striped8(idx):
    return np.concatenate([x.reshape(-1, 16).T for x in idx]).astype(np.uint16)


def runs(offs, k):
    lists = np.stack([offs[16 * r : 16 * r + 16].T.reshape(-1) for r in range(8)]).astype(np.int64)
    return lists[np.arange(k) % 512 // 64]


def pack_weight(w):
    k, n = w.shape
    w = f64(np.asarray(w, np.float32).astype(ml_dtypes.bfloat16)).reshape(k // 32, 32, n)
    amax = np.abs(w).max(1)
    byte = np.clip(np.where(amax > 0, np.frexp(amax)[1] - 1 + 127 - 7, 1), 1, 254)
    scaled = (w * np.exp2(127.0 - byte)[:, None, :]).reshape(k, n).astype(np.float32)
    words = np.ascontiguousarray(scaled.reshape(k // 512, 128, 4, n).transpose(0, 1, 3, 2)).astype(ml_dtypes.float8_e4m3fn).view(np.uint8)
    return words, np.ascontiguousarray(byte.astype(np.uint8).reshape(k // 512, 16, n))


def unpack_weight(words, scales):
    g, p, n, _ = words.shape
    vals = np.ascontiguousarray(words).view(ml_dtypes.float8_e4m3fn).astype(np.float64) * np.repeat(np.exp2(scales.astype(np.float64) - 127.0), 8, axis=1)[..., None]
    return vals.transpose(0, 1, 3, 2).reshape(g * 512, n)


def sigmoid(v):
    return 1.0 / (1.0 + np.exp(-np.maximum(v, -700.0)))


K, T, S, H, C = 512, 2048, 512, 512, 512


def setup_inputs():
    n = np.random.standard_normal
    s = mx_kscale(K)[:, None]
    packed_xT = pack_weight(n((K, T)) * s)
    return {
        "x_words": packed_xT[0],
        "x_scales": packed_xT[1],
        "w1": (n((K, H)) / np.sqrt(2 * K) / s).astype(np.float32),
        "w2": (n((K, H)) / np.sqrt(2 * K) / s).astype(np.float32),
        "gs": (np.random.uniform(0.5, 1.5, (K, 1)) / s).astype(np.float32),
        "sl": np.random.uniform(1.0, 2.0, (C, 1)).astype(np.float32),
        "th": (0.5 * n((C, 1))).astype(np.float32),
        "offs": striped(np.random.permutation(T)[:S]),
        "hz": striped8(np.random.randint(0, T, (8, S))),
        "n1": striped8(np.stack([np.random.permutation(S) for _ in range(8)])),
        "n2": striped8(np.stack([np.random.permutation(S) for _ in range(8)])),
        "cand": striped(np.random.permutation(T)[:C]),
        "n3": striped8(np.stack([np.random.permutation(S) for _ in range(8)])),
        "n4": striped8(np.stack([np.random.permutation(S) for _ in range(8)])),
    }


def reference(x_words, x_scales, w1, w2, gs, sl, th, offs, hz, n1, n2, cand, n3, n4):
    x_cand = unpack_weight(x_words, x_scales)[:, unstriped(cand)]
    xq = unpack_weight(x_words, x_scales)[:, unstriped(offs)]
    x_hz = unpack_weight(x_words, x_scales)[np.arange(K)[:, None], runs(hz, K)]
    y = mxq(f64(w1), 0, "e4m3").T @ xq + mxq(f64(w2), 0, "e4m3").T @ x_hz
    ds = np.zeros((H, S))
    ds[np.arange(H)[:, None], runs(n1, H)] = y
    ds2 = np.zeros((H, S))
    ds2[np.arange(H)[:, None], runs(n2, H)] = y
    z = f64(gs) * np.maximum(ds, ds2)
    s = 0.0625 * ((x_cand.T @ mxq(z, 0, "e4m3")))
    sg = sigmoid(f64(sl) * (s[np.arange(C)[:, None], runs(n3, C)] - f64(th)))
    st = s * sg
    return st - (0.5 * (st[np.arange(C)[:, None], runs(n4, C)]))

@@ -1,0 +1,209 @@
+from contextlib import ExitStack
+
+import concourse.mybir as mybir
+
+K, T, S, H, C = 512, 2048, 512, 512, 512
+FLOPS = 2 * K * H * S * 2 + 2 * H * C * S
+
+F32 = mybir.dt.float32
+BF16 = mybir.dt.bfloat16
+I32 = mybir.dt.int32
+U32 = mybir.dt.uint32
+U16 = mybir.dt.uint16
+U8 = mybir.dt.uint8
+FP8X4 = mybir.dt.float8_e4m3fn_x4
+ALU = mybir.AluOpType
+ACT = mybir.ActivationFunctionType
+
+P = 128
+PACK = 4
+HALF = S // 2
+LIST_COLS = S // 16
+WINDOW = 2 * S
+
+
+def tile_picked_thcsendtwoehp_none_p_kernel(
+    tc, x_words, x_scales, w1, w2, gs, sl, th, offs, hz, n1, n2, cand, n3, n4, out
+):
+    nc = tc.nc
+    with ExitStack() as ctx:
+        lists = ctx.enter_context(tc.tile_pool(name="lists", bufs=1))
+        keep = ctx.enter_context(tc.tile_pool(name="keep", bufs=1))
+        psum = ctx.enter_context(tc.psum_pool(name="psum", bufs=1))
+
+        def load_list(src, name):
+            tile = lists.tile([P, LIST_COLS], U16, name=name)
+            nc.sync.dma_start(tile[:], src)
+            return tile
+
+        def half_of(tile, h):
+            return tile[:, h * (LIST_COLS // 2) : (h + 1) * (LIST_COLS // 2)]
+
+        def cols(h):
+            return slice(h * HALF, (h + 1) * HALF)
+
+        scale_table = keep.tile([P, T], U8, align_bytes=64)
+        nc.gpsimd.memset(scale_table[:].bitcast(I32), 0)
+        planes = keep.tile([P, 3 * S], U8, align_bytes=64)
+        nc.vector.memset(planes[:].bitcast(I32), 0)
+        nc.scalar.dma_start(scale_table[0:P:8, :].bitcast(I32), x_scales[0].bitcast(I32))
+
+        hz_l = load_list(hz, "hz_l")
+        offs_l = load_list(offs, "offs_l")
+        w1_raw = keep.tile([P, PACK, H], F32)
+        nc.sync.dma_start(w1_raw[:], w1.rearrange("(p j) c -> p j c", j=PACK))
+        cand_l = load_list(cand, "cand_l")
+        n1_l = load_list(n1, "n1_l")
+        n2_l = load_list(n2, "n2_l")
+        n3_l = load_list(n3, "n3_l")
+        n4_l = load_list(n4, "n4_l")
+        word_table = keep.tile([P, T], I32, align_bytes=64)
+        nc.sync.dma_start(word_table[:], x_words[0].rearrange("p n r -> p (n r)").bitcast(I32))
+        w2_raw = []
+        for h in range(2):
+            part = keep.tile([P, PACK, H // 2], F32, name="w2_raw%d" % h)
+            nc.sync.dma_start(part[:], w2.rearrange("(p j) c -> p j c", j=PACK)[:, :, h * (H // 2) : (h + 1) * (H // 2)])
+            w2_raw.append(part)
+
+        gs_sb = keep.tile([P, PACK], F32)
+        sl_sb = keep.tile([P, PACK], F32)
+        th_sb = keep.tile([P, PACK], F32)
+        for tile, src in ((gs_sb, gs), (sl_sb, sl), (th_sb, th)):
+            nc.gpsimd.dma_start(tile[:], src.rearrange("(p t) o -> p (t o)", t=PACK))
+        sl_th = keep.tile([P, PACK], F32)
+        nc.gpsimd.tensor_tensor(sl_th[:], sl_sb[:], th_sb[:], ALU.mult)
+        bias_sb = keep.tile([P, PACK], F32)
+        nc.gpsimd.tensor_scalar(bias_sb[:], sl_th[:], -1.0, 0.0, ALU.mult, ALU.add)
+
+        picked_bytes = keep.tile([P, 3 * S], U8, align_bytes=64)
+        nc.vector.tensor_copy(picked_bytes[:, 0:S], scale_table[:].indirect(hz_l[:]))
+        nc.vector.tensor_copy(picked_bytes[:, S : 2 * S], scale_table[:].indirect(offs_l[:]))
+        nc.vector.tensor_copy(
+            picked_bytes[:, 2 * S : 3 * S].rearrange("p (t m) -> p m t", t=PACK), scale_table[:].indirect(cand_l[:])
+        )
+        for r in range(4):
+            nc.sync.dma_start(planes[r:P:32, :].bitcast(I32), picked_bytes[8 * r : P : 32, :].bitcast(I32))
+        hz_scale = planes[:, 0:S]
+        offs_scale = planes[:, S : 2 * S]
+        cand_scale = planes[:, 2 * S : 3 * S]
+
+        words = word_table[:].bitcast(U32)
+        offs_words = keep.tile([P, S], U32, align_bytes=64)
+        nc.vector.tensor_copy(offs_words[:], words.indirect(offs_l[:]))
+        hz_words = keep.tile([P, S], U32, align_bytes=64)
+        nc.vector.tensor_copy(hz_words[:], words.indirect(hz_l[:]))
+
+        def round_weights(dst, raw, t0, t1):
+            nc.scalar.copy(dst, raw.rearrange("p j (m t) -> p m t j", t=PACK)[:, :, t0:t1, :])
+
+        def by_tile(stage, n):
+            return stage.rearrange("p (t m j) -> p m t j", t=n, j=PACK)
+
+        def first_product(acc, wq1, ws1, wq2, ws2, span):
+            nc.tensor.matmul_mx(acc, lhsT=wq1.bitcast(FP8X4), lhsT_scale=ws1, rhs=offs_words[:, span].bitcast(FP8X4),
+                                rhs_scale=offs_scale[:, span], start=True, stop=False)
+            nc.tensor.matmul_mx(acc, lhsT=wq2.bitcast(FP8X4), lhsT_scale=ws2, rhs=hz_words[:, span].bitcast(FP8X4),
+                                rhs_scale=hz_scale[:, span], start=False, stop=True)
+
+        y_sb = [keep.tile([P, S], F32, name="y_sb%d" % t) for t in range(PACK)]
+
+        w1_bf = keep.tile([P, H * PACK], BF16, align_bytes=64)
+        round_weights(by_tile(w1_bf[:], PACK), w1_raw[:], 0, PACK)
+        w1_q = keep.tile([P, H], U32, align_bytes=64)
+        w1_s = keep.tile([P, H], U8, align_bytes=64)
+        nc.vector.quantize_mx(w1_q[:].bitcast(FP8X4), w1_s[:], w1_bf[:])
+
+        w2_bf_first = keep.tile([P, P * PACK], BF16, align_bytes=64, tag="slot_c")
+        w2_bf_rest = keep.tile([P, 3 * P * PACK], BF16, align_bytes=64)
+        for h in range(2):
+            m = slice(h * (P // 2), (h + 1) * (P // 2))
+            round_weights(by_tile(w2_bf_first[:], 1)[:, m], w2_raw[h][:], 0, 1)
+            round_weights(by_tile(w2_bf_rest[:], 3)[:, m], w2_raw[h][:], 1, PACK)
+        w2_q_first = keep.tile([P, P], U32, align_bytes=64)
+        w2_s_first = keep.tile([P, P], U8, align_bytes=64)
+        nc.vector.quantize_mx(w2_q_first[:].bitcast(FP8X4), w2_s_first[:], w2_bf_first[:])
+        for h in range(2):
+            acc = psum.tile([P, HALF], F32, name="y0_ps%d" % h, tag="bank%d" % h)
+            first_product(acc[:], w1_q[:, 0:P], w1_s[:, 0:P], w2_q_first[:], w2_s_first[:], cols(h))
+            nc.scalar.copy(y_sb[0][:, cols(h)], acc[:])
+
+        cand_words = keep.tile([P, C], U32, align_bytes=64, tag="slot_c")
+        nc.vector.tensor_copy(cand_words[:].rearrange("p (t m) -> p m t", t=PACK), words.indirect(cand_l[:]))
+
+        w2_q_rest = keep.tile([P, 3 * P], U32, align_bytes=64, tag="slot_a")
+        w2_s_rest = keep.tile([P, 3 * P], U8, align_bytes=64)
+        nc.vector.quantize_mx(w2_q_rest[:].bitcast(FP8X4), w2_s_rest[:], w2_bf_rest[:])
+        for t in range(1, PACK):
+            acc = psum.tile([P, S], F32, name="y%d_ps" % t, tag="bank%d" % (1 + t))
+            a = slice(t * P, (t + 1) * P)
+            b = slice((t - 1) * P, t * P)
+            first_product(acc[:], w1_q[:, a], w1_s[:, a], w2_q_rest[:, b], w2_s_rest[:, b], slice(0, S))
+            nc.scalar.copy(y_sb[t][:], acc[:])
+
+        z_bf = [keep.tile([P, HALF, PACK], BF16, align_bytes=64, name="z_bf%d" % h) for h in range(2)]
+        z_q = keep.tile([P, S], U32, align_bytes=64)
+        z_s = keep.tile([P, S], U8, align_bytes=64)
+        for t in range(PACK):
+            ds = keep.tile([P, WINDOW], F32, name="ds_%d" % t)
+            ds2 = keep.tile([P, WINDOW], F32, name="ds2_%d" % t)
+            if t == 0:
+                for h in range(2):
+                    nc.vector.tensor_copy(ds[:].indirect(half_of(n1_l, h)), y_sb[t][:, cols(h)])
+                    nc.vector.tensor_copy(ds2[:].indirect(half_of(n2_l, h)), y_sb[t][:, cols(h)])
+            else:
+                nc.vector.tensor_copy(ds[:].indirect(n1_l[:]), y_sb[t][:])
+                nc.vector.tensor_copy(ds2[:].indirect(n2_l[:]), y_sb[t][:])
+            larger = keep.tile([P, S], F32, name="larger%d" % t, align_bytes=64, tag=("slot_a", "larger1", "slot_d", "slot_d")[t])
+            if t < PACK - 1:
+                nc.vector.tensor_tensor(larger[:], ds[:, 0:S], ds2[:, 0:S], ALU.max)
+                for h in range(2):
+                    nc.scalar.activation(z_bf[h][:, :, t], larger[:, cols(h)], ACT.Copy, scale=gs_sb[:, t : t + 1])
+            else:
+                for h in range(2):
+                    nc.vector.tensor_tensor(larger[:, cols(h)], ds[:, cols(h)], ds2[:, cols(h)], ALU.max)
+                for h in range(2):
+                    nc.vector.tensor_scalar(z_bf[h][:, :, t], larger[:, cols(h)], gs_sb[:, t : t + 1], None, ALU.mult)
+        for h in range(2):
+            nc.vector.quantize_mx(z_q[:, cols(h)].bitcast(FP8X4), z_s[:, cols(h)], z_bf[h][:].rearrange("p c t -> p (c t)"))
+
+        def second_product(acc, t, span):
+            rows = slice(t * P, (t + 1) * P)
+            nc.tensor.matmul_mx(acc, lhsT=cand_words[:, rows].bitcast(FP8X4), lhsT_scale=cand_scale[:, rows],
+                                rhs=z_q[:, span].bitcast(FP8X4), rhs_scale=z_s[:, span], start=True, stop=True)
+
+        s_sb = [keep.tile([P, S], F32, name="s_sb%d" % t) for t in range(PACK)]
+        sg = [keep.tile([P, S], F32, name="sg%d" % t) for t in range(PACK)]
+        st = [keep.tile([P, S], F32, name="st%d" % t) for t in range(PACK)]
+        other = [keep.tile([P, S], F32, name="other%d" % t) for t in range(PACK)]
+        res = [keep.tile([P, S], F32, name="res%d" % t) for t in range(PACK)]
+        out_rows = out.rearrange("(p t) n -> p t n", t=PACK)
+
+        for h in range(2):
+            acc = psum.tile([P, HALF], F32, name="s0_ps%d" % h, tag="bank%d" % h)
+            second_product(acc[:], 0, cols(h))
+            nc.vector.tensor_scalar(s_sb[0][:, cols(h)], acc[:], 0.0625, None, ALU.mult)
+        for t in range(1, PACK):
+            acc = psum.tile([P, S], F32, name="s%d_ps" % t, tag="bank%d" % (1 + t))
+            second_product(acc[:], t, slice(0, S))
+            nc.vector.tensor_scalar(s_sb[t][:], acc[:], 0.0625, None, ALU.mult)
+
+        def gate(t):
+            for h in range(2):
+                nc.scalar.activation(sg[t][:, cols(h)], s_sb[t][:].indirect(half_of(n3_l, h)), ACT.Sigmoid,
+                                     bias=bias_sb[:, t : t + 1], scale=sl_sb[:, t : t + 1])
+            for h in range(2):
+                nc.vector.tensor_tensor(st[t][:, cols(h)], s_sb[t][:, cols(h)], sg[t][:, cols(h)], ALU.mult)
+
+        def finish(t):
+            for h in range(2):
+                nc.scalar.activation(other[t][:, cols(h)], st[t][:].indirect(half_of(n4_l, h)), ACT.Copy)
+            for h in range(2):
+                nc.vector.scalar_tensor_tensor(res[t][:, cols(h)], other[t][:, cols(h)], -0.5, st[t][:, cols(h)],
+                                               ALU.mult, ALU.add)
+                nc.sync.dma_start(out_rows[:, t, cols(h)], res[t][:, cols(h)])
+
+        gate(0)
+        for t in range(1, PACK):
+            gate(t)
+            finish(t - 1)
+        finish(PACK - 1)

@@ -1,6 +1,7 @@
 from contextlib import ExitStack
 
 import concourse.mybir as mybir
+from concourse.masks import make_identity
 
 K, T, S, H, C = 512, 2048, 512, 512, 512
 FLOPS = 2 * K * H * S * 2 + 2 * H * C * S
@@ -44,21 +45,23 @@ def tile_picked_thcsendtwoehp_none_p_kernel(
 
         scale_table = keep.tile([P, T], U8, align_bytes=64)
         nc.gpsimd.memset(scale_table[:].bitcast(I32), 0)
+        ident = keep.tile([P, P], F32)
+        make_identity(nc, ident[:])
         planes = keep.tile([P, 3 * S], U8, align_bytes=64)
         nc.vector.memset(planes[:].bitcast(I32), 0)
-        nc.scalar.dma_start(scale_table[0:P:8, :].bitcast(I32), x_scales[0].bitcast(I32))
 
         hz_l = load_list(hz, "hz_l")
         offs_l = load_list(offs, "offs_l")
-        w1_raw = keep.tile([P, PACK, H], F32)
-        nc.sync.dma_start(w1_raw[:], w1.rearrange("(p j) c -> p j c", j=PACK))
         cand_l = load_list(cand, "cand_l")
         n1_l = load_list(n1, "n1_l")
         n2_l = load_list(n2, "n2_l")
-        n3_l = load_list(n3, "n3_l")
-        n4_l = load_list(n4, "n4_l")
+        nc.sync.dma_start(scale_table[0:P:8, :].bitcast(I32), x_scales[0].bitcast(I32))
+        w1_raw = keep.tile([P, PACK, H], F32)
+        nc.sync.dma_start(w1_raw[:], w1.rearrange("(p j) c -> p j c", j=PACK))
         word_table = keep.tile([P, T], I32, align_bytes=64)
         nc.sync.dma_start(word_table[:], x_words[0].rearrange("p n r -> p (n r)").bitcast(I32))
+        n3_l = load_list(n3, "n3_l")
+        n4_l = load_list(n4, "n4_l")
         w2_raw = []
         for h in range(2):
             part = keep.tile([P, PACK, H // 2], F32, name="w2_raw%d" % h)
@@ -130,39 +133,78 @@ def tile_picked_thcsendtwoehp_none_p_kernel(
         cand_words = keep.tile([P, C], U32, align_bytes=64, tag="slot_c")
         nc.vector.tensor_copy(cand_words[:].rearrange("p (t m) -> p m t", t=PACK), words.indirect(cand_l[:]))
 
-        w2_q_rest = keep.tile([P, 3 * P], U32, align_bytes=64, tag="slot_a")
+        w2_q_rest = keep.tile([P, 3 * P], U32, align_bytes=64)
         w2_s_rest = keep.tile([P, 3 * P], U8, align_bytes=64)
         nc.vector.quantize_mx(w2_q_rest[:].bitcast(FP8X4), w2_s_rest[:], w2_bf_rest[:])
-        for t in range(1, PACK):
-            acc = psum.tile([P, S], F32, name="y%d_ps" % t, tag="bank%d" % (1 + t))
+
+        def make_y(t, bank):
+            acc = psum.tile([P, S], F32, name="y%d_ps" % t, tag=bank)
             a = slice(t * P, (t + 1) * P)
             b = slice((t - 1) * P, t * P)
             first_product(acc[:], w1_q[:, a], w1_s[:, a], w2_q_rest[:, b], w2_s_rest[:, b], slice(0, S))
             nc.scalar.copy(y_sb[t][:], acc[:])
 
+        make_y(2, "bank2")
+        make_y(3, "bank3")
+
+        def turn_and_add(acc, terms):
+            for c in range(S // P):
+                block = slice(c * P, (c + 1) * P)
+                for i, term in enumerate(terms):
+                    nc.tensor.matmul(acc[:, block], lhsT=term[:, block], rhs=ident[:], is_transpose=True,
+                                     start=(i == 0), stop=(i == len(terms) - 1))
+
         z_bf = [keep.tile([P, HALF, PACK], BF16, align_bytes=64, name="z_bf%d" % h) for h in range(2)]
         z_q = keep.tile([P, S], U32, align_bytes=64)
         z_s = keep.tile([P, S], U8, align_bytes=64)
-        for t in range(PACK):
-            ds = keep.tile([P, WINDOW], F32, name="ds_%d" % t)
-            ds2 = keep.tile([P, WINDOW], F32, name="ds2_%d" % t)
-            if t == 0:
+        order = (0, 2, 3, 1)
+        ds = {}
+        ds2 = {}
+        for t in order:
+            ds[t] = keep.tile([P, WINDOW], F32, name="ds_%d" % t)
+            ds2[t] = keep.tile([P, WINDOW], F32, name="ds2_%d" % t)
+
+        def scatter(t):
+            if t == order[0]:
                 for h in range(2):
-                    nc.vector.tensor_copy(ds[:].indirect(half_of(n1_l, h)), y_sb[t][:, cols(h)])
-                    nc.vector.tensor_copy(ds2[:].indirect(half_of(n2_l, h)), y_sb[t][:, cols(h)])
+                    nc.vector.tensor_copy(ds[t][:].indirect(half_of(n1_l, h)), y_sb[t][:, cols(h)])
+                    nc.vector.tensor_copy(ds2[t][:].indirect(half_of(n2_l, h)), y_sb[t][:, cols(h)])
             else:
-                nc.vector.tensor_copy(ds[:].indirect(n1_l[:]), y_sb[t][:])
-                nc.vector.tensor_copy(ds2[:].indirect(n2_l[:]), y_sb[t][:])
-            larger = keep.tile([P, S], F32, name="larger%d" % t, align_bytes=64, tag=("slot_a", "larger1", "slot_d", "slot_d")[t])
-            if t < PACK - 1:
-                nc.vector.tensor_tensor(larger[:], ds[:, 0:S], ds2[:, 0:S], ALU.max)
-                for h in range(2):
-                    nc.scalar.activation(z_bf[h][:, :, t], larger[:, cols(h)], ACT.Copy, scale=gs_sb[:, t : t + 1])
-            else:
-                for h in range(2):
-                    nc.vector.tensor_tensor(larger[:, cols(h)], ds[:, cols(h)], ds2[:, cols(h)], ALU.max)
-                for h in range(2):
-                    nc.vector.tensor_scalar(z_bf[h][:, :, t], larger[:, cols(h)], gs_sb[:, t : t + 1], None, ALU.mult)
+                nc.vector.tensor_copy(ds[t][:].indirect(n1_l[:]), y_sb[t][:])
+                nc.vector.tensor_copy(ds2[t][:].indirect(n2_l[:]), y_sb[t][:])
+
+        def negate(t):
+            minus_ds = keep.tile([P, S], F32, name="minus_ds")
+            nc.scalar.activation(minus_ds[:], ds[t][:, 0:S], ACT.Copy, scale=-1.0)
+            return minus_ds
+
+        scatter(order[0])
+        minus_ds = negate(order[0])
+        for i, t in enumerate(order[:-1]):
+            turned = psum.tile([P, S], F32, name="turned", tag="bank3")
+            turn_and_add(turned, [ds[t]])
+            ds_turned = keep.tile([P, S], F32, name="ds_turned")
+            nc.scalar.copy(ds_turned[:], turned[:])
+            gap = psum.tile([P, S], F32, name="gap", tag="bank3")
+            turn_and_add(gap, [minus_ds, ds2[t]])
+            excess = keep.tile([P, S], F32, name="excess")
+            nc.scalar.activation(excess[:], gap[:], ACT.Relu)
+            larger_ps = psum.tile([P, S], F32, name="larger_ps", tag="bank5")
+            turn_and_add(larger_ps, [ds_turned, excess])
+            if i + 2 < len(order):
+                scatter(order[i + 1])
+                minus_ds = negate(order[i + 1])
+            for h in range(2):
+                nc.scalar.activation(z_bf[h][:, :, t], larger_ps[:, cols(h)], ACT.Copy, scale=gs_sb[:, t : t + 1])
+            if i == 0:
+                make_y(order[-1], "bank5")
+        last = order[-1]
+        scatter(last)
+        larger = keep.tile([P, S], F32)
+        for h in range(2):
+            nc.vector.tensor_tensor(larger[:, cols(h)], ds[last][:, cols(h)], ds2[last][:, cols(h)], ALU.max)
+        for h in range(2):
+            nc.vector.tensor_scalar(z_bf[h][:, :, last], larger[:, cols(h)], gs_sb[:, last : last + 1], None, ALU.mult)
         for h in range(2):
             nc.vector.quantize_mx(z_q[:, cols(h)].bitcast(FP8X4), z_s[:, cols(h)], z_bf[h][:].rearrange("p c t -> p (c t)"))
 
@@ -171,39 +213,36 @@ def tile_picked_thcsendtwoehp_none_p_kernel(
             nc.tensor.matmul_mx(acc, lhsT=cand_words[:, rows].bitcast(FP8X4), lhsT_scale=cand_scale[:, rows],
                                 rhs=z_q[:, span].bitcast(FP8X4), rhs_scale=z_s[:, span], start=True, stop=True)
 
-        s_sb = [keep.tile([P, S], F32, name="s_sb%d" % t) for t in range(PACK)]
+        s_sb = [keep.tile([P, S], F32, name="s_sb%d" % t, tag="row%d" % t) for t in range(PACK)]
         sg = [keep.tile([P, S], F32, name="sg%d" % t) for t in range(PACK)]
         st = [keep.tile([P, S], F32, name="st%d" % t) for t in range(PACK)]
-        other = [keep.tile([P, S], F32, name="other%d" % t) for t in range(PACK)]
         res = [keep.tile([P, S], F32, name="res%d" % t) for t in range(PACK)]
         out_rows = out.rearrange("(p t) n -> p t n", t=PACK)
 
+        raw = []
         for h in range(2):
             acc = psum.tile([P, HALF], F32, name="s0_ps%d" % h, tag="bank%d" % h)
             second_product(acc[:], 0, cols(h))
-            nc.vector.tensor_scalar(s_sb[0][:, cols(h)], acc[:], 0.0625, None, ALU.mult)
+            nc.scalar.activation(s_sb[0][:, cols(h)], acc[:], ACT.Copy, scale=0.0625)
+            raw.append(acc[:])
         for t in range(1, PACK):
-            acc = psum.tile([P, S], F32, name="s%d_ps" % t, tag="bank%d" % (1 + t))
+            acc = psum.tile([P, S], F32, name="s%d_ps" % t, tag=("bank2", "bank6", "bank7")[t - 1])
             second_product(acc[:], t, slice(0, S))
             nc.vector.tensor_scalar(s_sb[t][:], acc[:], 0.0625, None, ALU.mult)
+            raw.extend([acc[:, cols(0)], acc[:, cols(1)]])
 
-        def gate(t):
+        for t in range(PACK):
             for h in range(2):
                 nc.scalar.activation(sg[t][:, cols(h)], s_sb[t][:].indirect(half_of(n3_l, h)), ACT.Sigmoid,
                                      bias=bias_sb[:, t : t + 1], scale=sl_sb[:, t : t + 1])
             for h in range(2):
-                nc.vector.tensor_tensor(st[t][:, cols(h)], s_sb[t][:, cols(h)], sg[t][:, cols(h)], ALU.mult)
+                nc.vector.scalar_tensor_tensor(st[t][:, cols(h)], raw[2 * t + h], 0.0625, sg[t][:, cols(h)],
+                                               ALU.mult, ALU.mult)
 
-        def finish(t):
-            for h in range(2):
-                nc.scalar.activation(other[t][:, cols(h)], st[t][:].indirect(half_of(n4_l, h)), ACT.Copy)
-            for h in range(2):
-                nc.vector.scalar_tensor_tensor(res[t][:, cols(h)], other[t][:, cols(h)], -0.5, st[t][:, cols(h)],
-                                               ALU.mult, ALU.add)
-                nc.sync.dma_start(out_rows[:, t, cols(h)], res[t][:, cols(h)])
-
-        gate(0)
-        for t in range(1, PACK):
-            gate(t)
-            finish(t - 1)
-        finish(PACK - 1)
+        for t in range(PACK):
+            other = keep.tile([P, S], F32, name="other%d" % t, tag="row%d" % ((t + 2) % PACK))
+            pieces = (0, 256, 512) if t < PACK - 1 else (0, 256, 384, 512)
+            for a, b in zip(pieces[:-1], pieces[1:]):
+                nc.scalar.activation(other[:, a:b], st[t][:].indirect(n4_l[:, a // 16 : b // 16]), ACT.Copy)
+                nc.vector.scalar_tensor_tensor(res[t][:, a:b], other[:, a:b], -0.5, st[t][:, a:b], ALU.mult, ALU.add)
+                nc.sync.dma_start(out_rows[:, t, a:b], res[t][:, a:b])

@@ -50,6 +50,11 @@ def tile_picked_thcsendtwoehp_none_p_kernel(
         planes = keep.tile([P, 3 * S], U8, align_bytes=64)
         nc.vector.memset(planes[:].bitcast(I32), 0)
 
+        warm_in = keep.tile([P, 1], F32)
+        nc.vector.memset(warm_in[:], 0.0)
+        warm_out = keep.tile([P, 1], F32)
+        nc.scalar.activation(warm_out[:], warm_in[:], ACT.Sigmoid)
+
         hz_l = load_list(hz, "hz_l")
         offs_l = load_list(offs, "offs_l")
         cand_l = load_list(cand, "cand_l")

@@ -37,6 +37,11 @@ def tile_picked_thcsendtwoehp_none_p_kernel(
             nc.sync.dma_start(tile[:], src)
             return tile
 
+        def load_column(src, name):
+            tile = keep.tile([P, PACK], F32, name=name)
+            nc.sync.dma_start(tile[:], src.rearrange("(p t) o -> p (t o)", t=PACK))
+            return tile
+
         def half_of(tile, h):
             return tile[:, h * (LIST_COLS // 2) : (h + 1) * (LIST_COLS // 2)]
 
@@ -50,6 +55,7 @@ def tile_picked_thcsendtwoehp_none_p_kernel(
         planes = keep.tile([P, 3 * S], U8, align_bytes=64)
         nc.vector.memset(planes[:].bitcast(I32), 0)
 
+
         warm_in = keep.tile([P, 1], F32)
         nc.vector.memset(warm_in[:], 0.0)
         warm_out = keep.tile([P, 1], F32)
@@ -58,13 +64,16 @@ def tile_picked_thcsendtwoehp_none_p_kernel(
         hz_l = load_list(hz, "hz_l")
         offs_l = load_list(offs, "offs_l")
         cand_l = load_list(cand, "cand_l")
-        n1_l = load_list(n1, "n1_l")
-        n2_l = load_list(n2, "n2_l")
+        gs_sb = load_column(gs, "gs_sb")
+        sl_sb = load_column(sl, "sl_sb")
         nc.sync.dma_start(scale_table[0:P:8, :].bitcast(I32), x_scales[0].bitcast(I32))
         w1_raw = keep.tile([P, PACK, H], F32)
         nc.sync.dma_start(w1_raw[:], w1.rearrange("(p j) c -> p j c", j=PACK))
         word_table = keep.tile([P, T], I32, align_bytes=64)
         nc.sync.dma_start(word_table[:], x_words[0].rearrange("p n r -> p (n r)").bitcast(I32))
+        th_sb = load_column(th, "th_sb")
+        n1_l = load_list(n1, "n1_l")
+        n2_l = load_list(n2, "n2_l")
         n3_l = load_list(n3, "n3_l")
         n4_l = load_list(n4, "n4_l")
         w2_raw = []
@@ -73,11 +82,6 @@ def tile_picked_thcsendtwoehp_none_p_kernel(
             nc.sync.dma_start(part[:], w2.rearrange("(p j) c -> p j c", j=PACK)[:, :, h * (H // 2) : (h + 1) * (H // 2)])
             w2_raw.append(part)
 
-        gs_sb = keep.tile([P, PACK], F32)
-        sl_sb = keep.tile([P, PACK], F32)
-        th_sb = keep.tile([P, PACK], F32)
-        for tile, src in ((gs_sb, gs), (sl_sb, sl), (th_sb, th)):
-            nc.gpsimd.dma_start(tile[:], src.rearrange("(p t) o -> p (t o)", t=PACK))
         sl_th = keep.tile([P, PACK], F32)
         nc.gpsimd.tensor_tensor(sl_th[:], sl_sb[:], th_sb[:], ALU.mult)
         bias_sb = keep.tile([P, PACK], F32)
@@ -153,7 +157,7 @@ def tile_picked_thcsendtwoehp_none_p_kernel(
         make_y(3, "bank3")
 
         def turn_and_add(acc, terms):
-            for c in range(S // P):
+            for c in range(acc.shape[1] // P):
                 block = slice(c * P, (c + 1) * P)
                 for i, term in enumerate(terms):
                     nc.tensor.matmul(acc[:, block], lhsT=term[:, block], rhs=ident[:], is_transpose=True,
@@ -178,31 +182,27 @@ def tile_picked_thcsendtwoehp_none_p_kernel(
                 nc.vector.tensor_copy(ds[t][:].indirect(n1_l[:]), y_sb[t][:])
                 nc.vector.tensor_copy(ds2[t][:].indirect(n2_l[:]), y_sb[t][:])
 
-        def negate(t):
-            minus_ds = keep.tile([P, S], F32, name="minus_ds")
-            nc.scalar.activation(minus_ds[:], ds[t][:, 0:S], ACT.Copy, scale=-1.0)
-            return minus_ds
-
-        scatter(order[0])
-        minus_ds = negate(order[0])
         for i, t in enumerate(order[:-1]):
+            scatter(t)
+            minus_ds = keep.tile([P, S], F32, name="minus_ds", tag="work")
+            nc.scalar.activation(minus_ds[:], ds[t][:, 0:S], ACT.Copy, scale=-1.0)
             turned = psum.tile([P, S], F32, name="turned", tag="bank3")
-            turn_and_add(turned, [ds[t]])
+            turn_and_add(turned, [ds[t][:, 0:S]])
             ds_turned = keep.tile([P, S], F32, name="ds_turned")
             nc.scalar.copy(ds_turned[:], turned[:])
-            gap = psum.tile([P, S], F32, name="gap", tag="bank3")
-            turn_and_add(gap, [minus_ds, ds2[t]])
-            excess = keep.tile([P, S], F32, name="excess")
-            nc.scalar.activation(excess[:], gap[:], ACT.Relu)
-            larger_ps = psum.tile([P, S], F32, name="larger_ps", tag="bank5")
-            turn_and_add(larger_ps, [ds_turned, excess])
-            if i + 2 < len(order):
-                scatter(order[i + 1])
-                minus_ds = negate(order[i + 1])
+            excess = []
             for h in range(2):
-                nc.scalar.activation(z_bf[h][:, :, t], larger_ps[:, cols(h)], ACT.Copy, scale=gs_sb[:, t : t + 1])
+                gap = psum.tile([P, HALF], F32, name="gap%d" % h, tag=("bank4", "bank3")[h])
+                turn_and_add(gap, [minus_ds[:, cols(h)], ds2[t][:, cols(h)]])
+                part = keep.tile([P, HALF], F32, name="excess%d" % h, tag=("excess0", "work")[h])
+                nc.scalar.activation(part[:], gap[:], ACT.Relu)
+                excess.append(part)
+            for h in range(2):
+                larger_ps = psum.tile([P, HALF], F32, name="larger_ps%d" % h, tag=("bank5", "bank6")[h])
+                turn_and_add(larger_ps, [ds_turned[:, cols(h)], excess[h][:]])
+                nc.scalar.activation(z_bf[h][:, :, t], larger_ps[:], ACT.Copy, scale=gs_sb[:, t : t + 1])
             if i == 0:
-                make_y(order[-1], "bank5")
+                make_y(order[-1], "bank6")
         last = order[-1]
         scatter(last)
         larger = keep.tile([P, S], F32)
@@ -231,7 +231,7 @@ def tile_picked_thcsendtwoehp_none_p_kernel(
             nc.scalar.activation(s_sb[0][:, cols(h)], acc[:], ACT.Copy, scale=0.0625)
             raw.append(acc[:])
         for t in range(1, PACK):
-            acc = psum.tile([P, S], F32, name="s%d_ps" % t, tag=("bank2", "bank6", "bank7")[t - 1])
+            acc = psum.tile([P, S], F32, name="s%d_ps" % t, tag=("bank2", "bank7", "bank4")[t - 1])
             second_product(acc[:], t, slice(0, S))
             nc.vector.tensor_scalar(s_sb[t][:], acc[:], 0.0625, None, ALU.mult)
             raw.extend([acc[:, cols(0)], acc[:, cols(1)]])

from contextlib import ExitStack

import concourse.mybir as mybir
from concourse.masks import make_identity

K, T, S, H, C = 512, 2048, 512, 512, 512
FLOPS = 2 * K * H * S * 2 + 2 * H * C * S

F32 = mybir.dt.float32
BF16 = mybir.dt.bfloat16
I32 = mybir.dt.int32
U32 = mybir.dt.uint32
U16 = mybir.dt.uint16
U8 = mybir.dt.uint8
FP8X4 = mybir.dt.float8_e4m3fn_x4
ALU = mybir.AluOpType
ACT = mybir.ActivationFunctionType

P = 128
PACK = 4
HALF = S // 2
LIST_COLS = S // 16
WINDOW = 2 * S


def tile_picked_thcsendtwoehp_none_p_kernel(
    tc, x_words, x_scales, w1, w2, gs, sl, th, offs, hz, n1, n2, cand, n3, n4, out
):
    nc = tc.nc
    with ExitStack() as ctx:
        lists = ctx.enter_context(tc.tile_pool(name="lists", bufs=1))
        keep = ctx.enter_context(tc.tile_pool(name="keep", bufs=1))
        psum = ctx.enter_context(tc.psum_pool(name="psum", bufs=1))

        def load_list(src, name):
            tile = lists.tile([P, LIST_COLS], U16, name=name)
            nc.sync.dma_start(tile[:], src)
            return tile

        def load_column(src, name):
            tile = keep.tile([P, PACK], F32, name=name)
            nc.sync.dma_start(tile[:], src.rearrange("(p t) o -> p (t o)", t=PACK))
            return tile

        def half_of(tile, h):
            return tile[:, h * (LIST_COLS // 2) : (h + 1) * (LIST_COLS // 2)]

        def cols(h):
            return slice(h * HALF, (h + 1) * HALF)

        scale_table = keep.tile([P, T], U8, align_bytes=64)
        nc.gpsimd.memset(scale_table[:].bitcast(I32), 0)
        ident = keep.tile([P, P], F32)
        make_identity(nc, ident[:])
        planes = keep.tile([P, 3 * S], U8, align_bytes=64)
        nc.vector.memset(planes[:].bitcast(I32), 0)


        warm_in = keep.tile([P, 1], F32)
        nc.vector.memset(warm_in[:], 0.0)
        warm_out = keep.tile([P, 1], F32)
        nc.scalar.activation(warm_out[:], warm_in[:], ACT.Sigmoid)

        hz_l = load_list(hz, "hz_l")
        offs_l = load_list(offs, "offs_l")
        cand_l = load_list(cand, "cand_l")
        gs_sb = load_column(gs, "gs_sb")
        sl_sb = load_column(sl, "sl_sb")
        nc.sync.dma_start(scale_table[0:P:8, :].bitcast(I32), x_scales[0].bitcast(I32))
        w1_raw = keep.tile([P, PACK, H], F32)
        nc.sync.dma_start(w1_raw[:], w1.rearrange("(p j) c -> p j c", j=PACK))
        word_table = keep.tile([P, T], I32, align_bytes=64)
        nc.sync.dma_start(word_table[:], x_words[0].rearrange("p n r -> p (n r)").bitcast(I32))
        th_sb = load_column(th, "th_sb")
        n1_l = load_list(n1, "n1_l")
        n2_l = load_list(n2, "n2_l")
        n3_l = load_list(n3, "n3_l")
        n4_l = load_list(n4, "n4_l")
        w2_raw = []
        for h in range(2):
            part = keep.tile([P, PACK, H // 2], F32, name="w2_raw%d" % h)
            nc.sync.dma_start(part[:], w2.rearrange("(p j) c -> p j c", j=PACK)[:, :, h * (H // 2) : (h + 1) * (H // 2)])
            w2_raw.append(part)

        sl_th = keep.tile([P, PACK], F32)
        nc.gpsimd.tensor_tensor(sl_th[:], sl_sb[:], th_sb[:], ALU.mult)
        bias_sb = keep.tile([P, PACK], F32)
        nc.gpsimd.tensor_scalar(bias_sb[:], sl_th[:], -1.0, 0.0, ALU.mult, ALU.add)

        picked_bytes = keep.tile([P, 3 * S], U8, align_bytes=64)
        nc.vector.tensor_copy(picked_bytes[:, 0:S], scale_table[:].indirect(hz_l[:]))
        nc.vector.tensor_copy(picked_bytes[:, S : 2 * S], scale_table[:].indirect(offs_l[:]))
        nc.vector.tensor_copy(
            picked_bytes[:, 2 * S : 3 * S].rearrange("p (t m) -> p m t", t=PACK), scale_table[:].indirect(cand_l[:])
        )
        for r in range(4):
            nc.sync.dma_start(planes[r:P:32, :].bitcast(I32), picked_bytes[8 * r : P : 32, :].bitcast(I32))
        hz_scale = planes[:, 0:S]
        offs_scale = planes[:, S : 2 * S]
        cand_scale = planes[:, 2 * S : 3 * S]

        words = word_table[:].bitcast(U32)
        offs_words = keep.tile([P, S], U32, align_bytes=64)
        nc.vector.tensor_copy(offs_words[:], words.indirect(offs_l[:]))
        hz_words = keep.tile([P, S], U32, align_bytes=64)
        nc.vector.tensor_copy(hz_words[:], words.indirect(hz_l[:]))

        def round_weights(dst, raw, t0, t1):
            nc.scalar.copy(dst, raw.rearrange("p j (m t) -> p m t j", t=PACK)[:, :, t0:t1, :])

        def by_tile(stage, n):
            return stage.rearrange("p (t m j) -> p m t j", t=n, j=PACK)

        def first_product(acc, wq1, ws1, wq2, ws2, span):
            nc.tensor.matmul_mx(acc, lhsT=wq1.bitcast(FP8X4), lhsT_scale=ws1, rhs=offs_words[:, span].bitcast(FP8X4),
                                rhs_scale=offs_scale[:, span], start=True, stop=False)
            nc.tensor.matmul_mx(acc, lhsT=wq2.bitcast(FP8X4), lhsT_scale=ws2, rhs=hz_words[:, span].bitcast(FP8X4),
                                rhs_scale=hz_scale[:, span], start=False, stop=True)

        y_sb = [keep.tile([P, S], F32, name="y_sb%d" % t) for t in range(PACK)]

        w1_bf = keep.tile([P, H * PACK], BF16, align_bytes=64)
        round_weights(by_tile(w1_bf[:], PACK), w1_raw[:], 0, PACK)
        w1_q = keep.tile([P, H], U32, align_bytes=64)
        w1_s = keep.tile([P, H], U8, align_bytes=64)
        nc.vector.quantize_mx(w1_q[:].bitcast(FP8X4), w1_s[:], w1_bf[:])

        w2_bf_first = keep.tile([P, P * PACK], BF16, align_bytes=64, tag="slot_c")
        w2_bf_rest = keep.tile([P, 3 * P * PACK], BF16, align_bytes=64)
        for h in range(2):
            m = slice(h * (P // 2), (h + 1) * (P // 2))
            round_weights(by_tile(w2_bf_first[:], 1)[:, m], w2_raw[h][:], 0, 1)
            round_weights(by_tile(w2_bf_rest[:], 3)[:, m], w2_raw[h][:], 1, PACK)
        w2_q_first = keep.tile([P, P], U32, align_bytes=64)
        w2_s_first = keep.tile([P, P], U8, align_bytes=64)
        nc.vector.quantize_mx(w2_q_first[:].bitcast(FP8X4), w2_s_first[:], w2_bf_first[:])
        for h in range(2):
            acc = psum.tile([P, HALF], F32, name="y0_ps%d" % h, tag="bank%d" % h)
            first_product(acc[:], w1_q[:, 0:P], w1_s[:, 0:P], w2_q_first[:], w2_s_first[:], cols(h))
            nc.scalar.copy(y_sb[0][:, cols(h)], acc[:])

        cand_words = keep.tile([P, C], U32, align_bytes=64, tag="slot_c")
        nc.vector.tensor_copy(cand_words[:].rearrange("p (t m) -> p m t", t=PACK), words.indirect(cand_l[:]))

        w2_q_rest = keep.tile([P, 3 * P], U32, align_bytes=64)
        w2_s_rest = keep.tile([P, 3 * P], U8, align_bytes=64)
        nc.vector.quantize_mx(w2_q_rest[:].bitcast(FP8X4), w2_s_rest[:], w2_bf_rest[:])

        def make_y(t, bank):
            acc = psum.tile([P, S], F32, name="y%d_ps" % t, tag=bank)
            a = slice(t * P, (t + 1) * P)
            b = slice((t - 1) * P, t * P)
            first_product(acc[:], w1_q[:, a], w1_s[:, a], w2_q_rest[:, b], w2_s_rest[:, b], slice(0, S))
            nc.scalar.copy(y_sb[t][:], acc[:])

        make_y(2, "bank2")
        make_y(3, "bank3")

        def turn_and_add(acc, terms):
            for c in range(acc.shape[1] // P):
                block = slice(c * P, (c + 1) * P)
                for i, term in enumerate(terms):
                    nc.tensor.matmul(acc[:, block], lhsT=term[:, block], rhs=ident[:], is_transpose=True,
                                     start=(i == 0), stop=(i == len(terms) - 1))

        z_bf = [keep.tile([P, HALF, PACK], BF16, align_bytes=64, name="z_bf%d" % h) for h in range(2)]
        z_q = keep.tile([P, S], U32, align_bytes=64)
        z_s = keep.tile([P, S], U8, align_bytes=64)
        order = (0, 2, 3, 1)
        ds = {}
        ds2 = {}
        for t in order:
            ds[t] = keep.tile([P, WINDOW], F32, name="ds_%d" % t)
            ds2[t] = keep.tile([P, WINDOW], F32, name="ds2_%d" % t)

        def scatter(t):
            if t == order[0]:
                for h in range(2):
                    nc.vector.tensor_copy(ds[t][:].indirect(half_of(n1_l, h)), y_sb[t][:, cols(h)])
                    nc.vector.tensor_copy(ds2[t][:].indirect(half_of(n2_l, h)), y_sb[t][:, cols(h)])
            else:
                nc.vector.tensor_copy(ds[t][:].indirect(n1_l[:]), y_sb[t][:])
                nc.vector.tensor_copy(ds2[t][:].indirect(n2_l[:]), y_sb[t][:])

        for i, t in enumerate(order[:-1]):
            scatter(t)
            minus_ds = keep.tile([P, S], F32, name="minus_ds", tag="work")
            nc.scalar.activation(minus_ds[:], ds[t][:, 0:S], ACT.Copy, scale=-1.0)
            turned = psum.tile([P, S], F32, name="turned", tag="bank3")
            turn_and_add(turned, [ds[t][:, 0:S]])
            ds_turned = keep.tile([P, S], F32, name="ds_turned")
            nc.scalar.copy(ds_turned[:], turned[:])
            excess = []
            for h in range(2):
                gap = psum.tile([P, HALF], F32, name="gap%d" % h, tag=("bank4", "bank3")[h])
                turn_and_add(gap, [minus_ds[:, cols(h)], ds2[t][:, cols(h)]])
                part = keep.tile([P, HALF], F32, name="excess%d" % h, tag=("excess0", "work")[h])
                nc.scalar.activation(part[:], gap[:], ACT.Relu)
                excess.append(part)
            for h in range(2):
                larger_ps = psum.tile([P, HALF], F32, name="larger_ps%d" % h, tag=("bank5", "bank6")[h])
                turn_and_add(larger_ps, [ds_turned[:, cols(h)], excess[h][:]])
                nc.scalar.activation(z_bf[h][:, :, t], larger_ps[:], ACT.Copy, scale=gs_sb[:, t : t + 1])
            if i == 0:
                make_y(order[-1], "bank6")
        last = order[-1]
        scatter(last)
        larger = keep.tile([P, S], F32)
        for h in range(2):
            nc.vector.tensor_tensor(larger[:, cols(h)], ds[last][:, cols(h)], ds2[last][:, cols(h)], ALU.max)
        for h in range(2):
            nc.vector.tensor_scalar(z_bf[h][:, :, last], larger[:, cols(h)], gs_sb[:, last : last + 1], None, ALU.mult)
        for h in range(2):
            nc.vector.quantize_mx(z_q[:, cols(h)].bitcast(FP8X4), z_s[:, cols(h)], z_bf[h][:].rearrange("p c t -> p (c t)"))

        def second_product(acc, t, span):
            rows = slice(t * P, (t + 1) * P)
            nc.tensor.matmul_mx(acc, lhsT=cand_words[:, rows].bitcast(FP8X4), lhsT_scale=cand_scale[:, rows],
                                rhs=z_q[:, span].bitcast(FP8X4), rhs_scale=z_s[:, span], start=True, stop=True)

        s_sb = [keep.tile([P, S], F32, name="s_sb%d" % t, tag="row%d" % t) for t in range(PACK)]
        sg = [keep.tile([P, S], F32, name="sg%d" % t) for t in range(PACK)]
        st = [keep.tile([P, S], F32, name="st%d" % t) for t in range(PACK)]
        res = [keep.tile([P, S], F32, name="res%d" % t) for t in range(PACK)]
        out_rows = out.rearrange("(p t) n -> p t n", t=PACK)

        raw = []
        for h in range(2):
            acc = psum.tile([P, HALF], F32, name="s0_ps%d" % h, tag="bank%d" % h)
            second_product(acc[:], 0, cols(h))
            nc.scalar.activation(s_sb[0][:, cols(h)], acc[:], ACT.Copy, scale=0.0625)
            raw.append(acc[:])
        for t in range(1, PACK):
            acc = psum.tile([P, S], F32, name="s%d_ps" % t, tag=("bank2", "bank7", "bank4")[t - 1])
            second_product(acc[:], t, slice(0, S))
            nc.vector.tensor_scalar(s_sb[t][:], acc[:], 0.0625, None, ALU.mult)
            raw.extend([acc[:, cols(0)], acc[:, cols(1)]])

        for t in range(PACK):
            for h in range(2):
                nc.scalar.activation(sg[t][:, cols(h)], s_sb[t][:].indirect(half_of(n3_l, h)), ACT.Sigmoid,
                                     bias=bias_sb[:, t : t + 1], scale=sl_sb[:, t : t + 1])
            for h in range(2):
                nc.vector.scalar_tensor_tensor(st[t][:, cols(h)], raw[2 * t + h], 0.0625, sg[t][:, cols(h)],
                                               ALU.mult, ALU.mult)

        for t in range(PACK):
            other = keep.tile([P, S], F32, name="other%d" % t, tag="row%d" % ((t + 2) % PACK))
            pieces = (0, 256, 512) if t < PACK - 1 else (0, 256, 384, 512)
            for a, b in zip(pieces[:-1], pieces[1:]):
                nc.scalar.activation(other[:, a:b], st[t][:].indirect(n4_l[:, a // 16 : b // 16]), ACT.Copy)
                nc.vector.scalar_tensor_tensor(res[t][:, a:b], other[:, a:b], -0.5, st[t][:, a:b], ALU.mult, ALU.add)
                nc.sync.dma_start(out_rows[:, t, a:b], res[t][:, a:b])
